import numpy as np
import ml_dtypes


def mxq(x, axis, fmt="e4m3"):
    dtype, down = {"e4m3": (ml_dtypes.float8_e4m3fn, 7), "e5m2": (ml_dtypes.float8_e5m2, 14)}[fmt]
    v = np.moveaxis(np.asarray(x, np.float32).astype(ml_dtypes.bfloat16).astype(np.float64), axis, -1)
    blocks = v.reshape(v.shape[:-1] + (-1, 32))
    amax = np.abs(blocks).max(-1, keepdims=True)
    byte = np.maximum(np.where(amax > 0, np.frexp(amax)[1] - 1 + 127, 0) - down, 1)
    scale = np.exp2(byte - 127.0)
    codes = (blocks / scale).astype(np.float32).astype(dtype).astype(np.float64)
    return np.moveaxis((codes * scale).reshape(v.shape), -1, axis)


WIDE = False


def mx_kscale(k):
    if not WIDE:
        return np.ones(k)
    levels = np.array([30, -30])
    if k % 512:
        return np.exp2(np.random.permutation(np.resize(levels, k // 32))).repeat(32)
    a = np.empty((k // 512, 16))
    for p in range(k // 512):
        a[p, :8] = np.random.permutation(np.resize(levels, 8))
        for g in range(8):
            far = levels[np.abs(levels - a[p, g]) >= 10]
            a[p, g + 8] = far[np.random.randint(len(far))]
    return np.exp2(a.ravel()).repeat(32)


def f64(x):
    return np.asarray(x).astype(np.float64)


def striped(idx):
    return np.tile(np.asarray(idx).reshape(-1, 16).T, (8, 1)).astype(np.uint16)


def unstriped(offs):
    return offs[:16].T.reshape(-1).astype(np.int64)


E2M1 = np.array([0.0, 0.5, 1.0, 1.5, 2.0, 3.0, 4.0, 6.0, -0.0, -0.5, -1.0, -1.5, -2.0, -3.0, -4.0, -6.0])


def pack_weight(w, fmt):
    k, n = w.shape
    w = f64(np.asarray(w, np.float32).astype(ml_dtypes.bfloat16)).reshape(k // 32, 32, n)
    amax = np.abs(w).max(1)
    if fmt in ("e4m3", "e5m2"):
        byte = np.frexp(amax)[1] - 1 + 127 - (7 if fmt == "e4m3" else 14)
    else:
        mant, ex = np.frexp(amax / 6.0)
        byte = np.where(mant > 0.5, ex, ex - 1) + 127
    byte = np.clip(np.where(amax > 0, byte, 1), 1, 254)
    scaled = (w * np.exp2(127.0 - byte)[:, None, :]).reshape(k, n).astype(np.float32)
    by_word = np.ascontiguousarray(scaled.reshape(k // 512, 128, 4, n).transpose(0, 1, 3, 2))
    if fmt in ("e4m3", "e5m2"):
        words = by_word.astype(ml_dtypes.float8_e4m3fn if fmt == "e4m3" else ml_dtypes.float8_e5m2).view(np.uint8)
    else:
        c = by_word.astype(ml_dtypes.float4_e2m1fn).view(np.uint8) & 0xF
        words = (c[..., 0::2] | (c[..., 1::2] << 4)).reshape(k // 512, 128, 2 * n)
    return np.ascontiguousarray(words), np.ascontiguousarray(byte.astype(np.uint8).reshape(k // 512, 16, n))


def unpack_weight(words, scales, fmt):
    g, _, n = scales.shape
    words = np.ascontiguousarray(words).reshape(g, 128, n, -1)
    if fmt in ("e4m3", "e5m2"):
        vals = words.view(ml_dtypes.float8_e4m3fn if fmt == "e4m3" else ml_dtypes.float8_e5m2).astype(np.float64)
    else:
        nib = np.empty((g, 128, n, 4), np.uint8)
        nib[..., 0::2] = words & 0xF
        nib[..., 1::2] = words >> 4
        vals = E2M1[nib]
    vals = vals * np.repeat(np.exp2(scales.astype(np.float64) - 127.0), 8, axis=1)[..., None]
    return vals.transpose(0, 1, 3, 2).reshape(g * 512, n)


def bf(x):
    return np.asarray(x, np.float32).astype(ml_dtypes.bfloat16)


def planes(Y):
    r, m = Y.shape
    b = f64(bf(Y)).reshape(r // 32, 32, m)
    amax = np.abs(b).max(1)
    byte = np.clip(np.where(amax > 0, np.frexp(amax)[1] - 1 + 127 - 7, 1), 1, 254)
    codes = (b * np.exp2(127.0 - byte)[:, None, :]).reshape(r, m).astype(np.float32).astype(ml_dtypes.float8_e4m3fn).view(np.uint8)
    words = codes.reshape(r // 512, 128, 4, m).transpose(0, 1, 3, 2)
    return np.ascontiguousarray(words), np.ascontiguousarray(byte.astype(np.uint8).reshape(r // 512, 16, m))


K, T, J, R, V, N, Q = 1024, 512, 128, 512, 512, 512, 64


def setup_inputs():
    n = np.random.standard_normal
    idx = np.random.permutation(T)[:J]
    idx2 = np.random.permutation(V)[:J]
    fk = mx_kscale(K)
    fr = mx_kscale(R)
    wp = pack_weight(n((K, R)) * 1 / np.sqrt(K) * fk[:, None] * fr, "e5m2")
    wbp = pack_weight(n((R, N)) * 1 / np.sqrt(R) / fr[:, None], "e2m1")
    return {
        "xf": (n((K, T))).astype(np.float32),
        "fk": (np.random.uniform(0.5, 2.0, (K, 1)) / fk[:, None]).astype(np.float32),
        "w_words": wp[0],
        "w_scales": wp[1],
        "tb": (n((R, V)) * 0.7 * fr[:, None]).astype(np.float32),
        "wb_words": wbp[0],
        "wb_scales": wbp[1],
        "rw": (np.random.uniform(0.5, 2.0, (1, J))).astype(np.float32),
        "qw": (np.random.uniform(0.5, 2.0, (1, Q))).astype(np.float32),
        "offs": striped(idx),
        "offs2": striped(idx2),
    }


def reference(xf, fk, w_words, w_scales, tb, wb_words, wb_scales, rw, qw, offs, offs2):
    idx = unstriped(offs)
    idx2 = unstriped(offs2)
    wu = unpack_weight(w_words, w_scales, "e5m2")
    wbu = unpack_weight(wb_words, wb_scales, "e2m1")
    xg = f64(xf)[:, idx]
    x1 = np.pad(xg, ((0, 0), (1, 0)))[:, :J]
    u = (xg - 0.6 * x1) * f64(fk)
    uq = mxq(u, 0, "e5m2")
    a = wu.T @ uq
    hid = np.maximum(a, f64(tb)[:, idx2])
    hidq = mxq(hid, 0, "e5m2")
    p = wbu.T @ hidq
    y = (p * f64(rw)).reshape(N, Q, J // Q).sum(axis=2) * f64(qw)
    words, scales = planes(y)
    return y, words, scales

@@ -1,0 +1,210 @@
+from contextlib import ExitStack
+
+import concourse.mybir as mybir
+
+K, T, J, R, V, N, Q = 1024, 512, 128, 512, 512, 512, 64
+FLOPS = 2 * K * R * J + 2 * R * N * J
+
+F32 = mybir.dt.float32
+BF16 = mybir.dt.bfloat16
+I32 = mybir.dt.int32
+U32 = mybir.dt.uint32
+U16 = mybir.dt.uint16
+U8 = mybir.dt.uint8
+E5M2 = mybir.dt.float8_e5m2_x4
+E4M3 = mybir.dt.float8_e4m3fn_x4
+E2M1 = mybir.dt.float4_e2m1fn_x4
+ALU = mybir.AluOpType
+COPY = mybir.ActivationFunctionType.Copy
+
+P = 128
+PACK = 4
+PASSES = K // (P * PACK)
+PAD = 8
+
+
+def walk_planes(ap):
+    return ap.rearrange("p t (c i) -> p c t i", i=4)
+
+
+def walk_words(ap):
+    return ap.rearrange("p (c i) t -> p c t i", i=4)
+
+
+def tile_list_steps_abovetable_groupsums_pl_kernel(
+    tc, xf, fk, w_words, w_scales, tb, wb_words, wb_scales, rw, qw, offs, offs2, out_0, out_1, out_2
+):
+    nc = tc.nc
+    with ExitStack() as ctx:
+        keep = ctx.enter_context(tc.tile_pool(name="keep", bufs=1))
+        psum = ctx.enter_context(tc.psum_pool(name="psum", bufs=1))
+
+        token_list = keep.tile([P, J // 16], U16, name="token_list")
+        entry_list = keep.tile([P, J // 16], U16, name="entry_list")
+        w_raw = [keep.tile([P, R], I32, name="w_raw_%d" % z, align_bytes=64) for z in range(PASSES)]
+        ws_raw = keep.tile([P, PASSES, R], U8, name="ws_raw", align_bytes=64)
+        wb_raw = keep.tile([P, 2 * N], U8, name="wb_raw", align_bytes=64)
+        wbs_raw = keep.tile([P, N], U8, name="wbs_raw", align_bytes=64)
+        fk_sb = keep.tile([P, PASSES, PACK], F32, name="fk_sb")
+        rw_sb = keep.tile([P, J], F32, name="rw_sb")
+        qw_sb = keep.tile([P, Q], F32, name="qw_sb")
+        x_rows = [[keep.tile([P, 2, T], F32, name="x_rows_%d_%d" % (z, h)) for h in range(2)] for z in range(PASSES)]
+        tb_rows = [keep.tile([P, 2, V], F32, name="tb_rows_%d" % h) for h in range(2)]
+        xg = [keep.tile([P, PACK, PAD + J], F32, name="xg_%d" % z) for z in range(PASSES)]
+
+        nc.gpsimd.memset(ws_raw[:].rearrange("p z c -> p (z c)").bitcast(I32), 0)
+        nc.gpsimd.memset(wbs_raw[:].bitcast(I32), 0)
+        nc.vector.memset(xg[0][:, :, 0:PAD], 0.0)
+        nc.scalar.activation(xg[1][:, :, 0:PAD], xg[0][:, :, 0:PAD], COPY)
+
+        xf_v = xf.rearrange("(z p t) c -> z p t c", z=PASSES, t=PACK)
+        tb_v = tb.rearrange("(p t) c -> p t c", t=PACK)
+
+        nc.sync.dma_start(token_list[:], offs)
+        nc.sync.dma_start(w_raw[0][:], w_words[0].rearrange("p c b -> p (c b)").bitcast(I32))
+        for g in range(4):
+            nc.sync.dma_start(
+                ws_raw[32 * g : 32 * g + 4, :, :].bitcast(I32),
+                w_scales[:, 4 * g : 4 * g + 4, :].rearrange("z r c -> r z c").bitcast(I32),
+            )
+        nc.sync.dma_start(x_rows[0][0][:], xf_v[0, :, 0:2, :])
+        nc.sync.dma_start(x_rows[0][1][:], xf_v[0, :, 2:4, :])
+        nc.sync.dma_start(x_rows[1][0][:], xf_v[1, :, 0:2, :])
+        for g in range(4):
+            nc.sync.dma_start(
+                wbs_raw[32 * g : 32 * g + 4, :].bitcast(I32), wb_scales[0, 4 * g : 4 * g + 4, :].bitcast(I32)
+            )
+        nc.sync.dma_start(x_rows[1][1][:], xf_v[1, :, 2:4, :])
+        nc.sync.dma_start(w_raw[1][:], w_words[1].rearrange("p c b -> p (c b)").bitcast(I32))
+        nc.sync.dma_start(wb_raw[:].bitcast(I32), wb_words[0].bitcast(I32))
+        nc.sync.dma_start(entry_list[:], offs2)
+        for h in range(2):
+            nc.sync.dma_start(tb_rows[h][:], tb_v[:, 2 * h : 2 * h + 2, :])
+        nc.gpsimd.dma_start(fk_sb[:], fk.rearrange("(z p t) o -> p z (t o)", z=PASSES, t=PACK))
+        nc.gpsimd.dma_start(rw_sb[:], rw.to_broadcast([P, J]))
+        nc.gpsimd.dma_start(qw_sb[:], qw.to_broadcast([P, Q]))
+
+        w_dealt = [keep.tile([P, PACK, P], I32, name="w_dealt_%d" % z, align_bytes=64) for z in range(PASSES)]
+        ws_dealt = keep.tile([P, PASSES, PACK, P], U8, name="ws_dealt", align_bytes=64)
+        wb_dealt = keep.tile([P, PACK, P, 2], U8, name="wb_dealt", align_bytes=64)
+        wbs_dealt = keep.tile([P, PACK, P], U8, name="wbs_dealt", align_bytes=64)
+        nc.vector.tensor_copy(
+            ws_dealt[:].rearrange("p z t m -> p z m t"), ws_raw[:].rearrange("p z (m t) -> p z m t", t=PACK)
+        )
+
+        a_bank = psum.tile([P, PACK, J], F32, name="a_bank")
+        steps = [keep.tile([P, PACK, J], F32, name="steps_%d" % z) for z in range(PASSES)]
+        u_bf = [keep.tile([P, J, PACK], BF16, name="u_bf_%d" % z, align_bytes=64) for z in range(PASSES)]
+        u_codes = [keep.tile([P, J], U32, name="u_codes_%d" % z, align_bytes=64) for z in range(PASSES)]
+        u_scales = [keep.tile([P, J], U8, name="u_scales_%d" % z, align_bytes=64) for z in range(PASSES)]
+
+        def first_stage(z):
+            for h in range(2):
+                for i in range(2):
+                    picked = x_rows[z][h][:, i, :].indirect(token_list[:])
+                    dst = xg[z][:, 2 * h + i, PAD : PAD + J]
+                    if (z, h, i) == (PASSES - 1, 1, 1):
+                        nc.vector.tensor_copy(dst, picked)
+                    else:
+                        nc.scalar.activation(dst, picked, COPY)
+                rows = slice(2 * h, 2 * h + 2)
+                nc.vector.scalar_tensor_tensor(
+                    steps[z][:, rows, :],
+                    xg[z][:, rows, PAD - 1 : PAD - 1 + J],
+                    -0.6,
+                    xg[z][:, rows, PAD : PAD + J],
+                    ALU.mult,
+                    ALU.add,
+                )
+            nc.vector.tensor_tensor(
+                walk_words(u_bf[z][:]),
+                walk_planes(steps[z][:]),
+                fk_sb[:, z, :].unsqueeze(1).unsqueeze(3).to_broadcast([P, J // 4, PACK, 4]),
+                ALU.mult,
+            )
+            nc.vector.quantize_mx(
+                u_codes[z][:].bitcast(E5M2), u_scales[z][:], u_bf[z][:].rearrange("p j t -> p (j t)")
+            )
+            nc.vector.tensor_copy(
+                w_dealt[z][:].rearrange("p t m -> p m t"), w_raw[z][:].rearrange("p (m t) -> p m t", t=PACK)
+            )
+            for t in range(PACK):
+                nc.tensor.matmul_mx(
+                    a_bank[:, t, :],
+                    lhsT=w_dealt[z][:, t, :].bitcast(E5M2),
+                    lhsT_scale=ws_dealt[:, z, t, :],
+                    rhs=u_codes[z][:].bitcast(E5M2),
+                    rhs_scale=u_scales[z][:],
+                    start=(z == 0 and t == 0),
+                    stop=(z == PASSES - 1 and t == PACK - 1),
+                )
+
+        first_stage(0)
+        nc.vector.tensor_copy(
+            wbs_dealt[:].rearrange("p t m -> p m t"), wbs_raw[:].rearrange("p (m t) -> p m t", t=PACK)
+        )
+        slot_weight = keep.tile([P, Q, 2], F32, name="slot_weight")
+        nc.gpsimd.tensor_tensor(
+            slot_weight[:],
+            rw_sb[:].rearrange("p (q e) -> p q e", e=2),
+            qw_sb[:].unsqueeze(2).to_broadcast([P, Q, 2]),
+            ALU.mult,
+        )
+        first_stage(1)
+        nc.vector.tensor_copy(
+            wb_dealt[:].rearrange("p t m b -> p m t b"), wb_raw[:].rearrange("p (m t b) -> p m t b", t=PACK, b=2)
+        )
+
+        tbg = keep.tile([P, PACK, J], F32, name="tbg")
+        for h in range(2):
+            for i in range(2):
+                picked = tb_rows[h][:, i, :].indirect(entry_list[:])
+                if (h, i) == (1, 1):
+                    nc.vector.tensor_copy(tbg[:, 2 * h + i, :], picked)
+                else:
+                    nc.scalar.activation(tbg[:, 2 * h + i, :], picked, COPY)
+
+        hid_bf = keep.tile([P, J, PACK], BF16, name="hid_bf", align_bytes=64)
+        hid_codes = keep.tile([P, J], U32, name="hid_codes", align_bytes=64)
+        hid_scales = keep.tile([P, J], U8, name="hid_scales", align_bytes=64)
+        nc.vector.tensor_tensor(walk_words(hid_bf[:]), walk_planes(a_bank[:]), walk_planes(tbg[:]), ALU.max)
+        nc.vector.quantize_mx(hid_codes[:].bitcast(E5M2), hid_scales[:], hid_bf[:].rearrange("p j t -> p (j t)"))
+
+        weighted = keep.tile([P, 2, 2, Q, 2], F32, name="weighted")
+        for h in range(2):
+            p_bank = psum.tile([P, 2, J], F32, name="p_bank_%d" % h)
+            for i in range(2):
+                t = 2 * h + i
+                nc.tensor.matmul_mx(
+                    p_bank[:, i, :],
+                    lhsT=wb_dealt[:, t, :, :].rearrange("p m b -> p (m b)").bitcast(E2M1),
+                    lhsT_scale=wbs_dealt[:, t, :],
+                    rhs=hid_codes[:].bitcast(E5M2),
+                    rhs_scale=hid_scales[:],
+                    start=True,
+                    stop=True,
+                )
+            nc.vector.tensor_tensor(
+                weighted[:, h, :, :, :],
+                p_bank[:].rearrange("p i (q e) -> p e q i", e=2),
+                slot_weight[:].rearrange("p q e -> p e q").unsqueeze(3).to_broadcast([P, 2, Q, 2]),
+                ALU.mult,
+            )
+
+        y_bf = keep.tile([P, Q, 2, 2], BF16, name="y_bf", align_bytes=64)
+        y = keep.tile([P, 2, 2, Q], F32, name="y")
+        y_codes = keep.tile([P, Q], U32, name="y_codes", align_bytes=64)
+        y_scales = keep.tile([P, Q], U8, name="y_scales", align_bytes=64)
+        even = weighted[:, :, 0, :, :].rearrange("p h q i -> p q h i")
+        odd = weighted[:, :, 1, :, :].rearrange("p h q i -> p q h i")
+        nc.vector.tensor_tensor(y_bf[:], even, odd, ALU.add)
+        nc.vector.tensor_tensor(y[:].rearrange("p h i q -> p q h i"), even, odd, ALU.add)
+        nc.vector.quantize_mx(y_codes[:].bitcast(E4M3), y_scales[:], y_bf[:].rearrange("p q h i -> p (q h i)"))
+
+        nc.sync.dma_start(out_0.rearrange("(p t) q -> p (t q)", t=PACK), y[:].rearrange("p h i q -> p (h i q)"))
+        nc.scalar.dma_start(out_1[0].rearrange("p c b -> p (c b)").bitcast(I32), y_codes[:].bitcast(I32))
+        for g in range(4):
+            queue = nc.sync if g % 2 == 0 else nc.scalar
+            queue.dma_start(
+                out_2[0, 4 * g : 4 * g + 4, :].bitcast(I32), y_scales[32 * g : 32 * g + 4, :].bitcast(I32)
+            )

@@ -1,6 +1,7 @@
 from contextlib import ExitStack
 
 import concourse.mybir as mybir
+from concourse.masks import make_identity
 
 K, T, J, R, V, N, Q = 1024, 512, 128, 512, 512, 512, 64
 FLOPS = 2 * K * R * J + 2 * R * N * J
@@ -21,6 +22,8 @@ P = 128
 PACK = 4
 PASSES = K // (P * PACK)
 PAD = 8
+TB_PIECES = ((0, 2), (2, 3), (3, 4))
+X_PIECES = (((0, 2), (2, 4)), ((0, 2), (2, 3), (3, 4)))
 
 
 def walk_planes(ap):
@@ -41,19 +44,25 @@ def tile_list_steps_abovetable_groupsums_pl_kernel(
 
         token_list = keep.tile([P, J // 16], U16, name="token_list")
         entry_list = keep.tile([P, J // 16], U16, name="entry_list")
-        w_raw = [keep.tile([P, R], I32, name="w_raw_%d" % z, align_bytes=64) for z in range(PASSES)]
+        w_raw = keep.tile([P, PASSES, R], I32, name="w_raw", align_bytes=64)
         ws_raw = keep.tile([P, PASSES, R], U8, name="ws_raw", align_bytes=64)
         wb_raw = keep.tile([P, 2 * N], U8, name="wb_raw", align_bytes=64)
         wbs_raw = keep.tile([P, N], U8, name="wbs_raw", align_bytes=64)
         fk_sb = keep.tile([P, PASSES, PACK], F32, name="fk_sb")
-        rw_sb = keep.tile([P, J], F32, name="rw_sb")
-        qw_sb = keep.tile([P, Q], F32, name="qw_sb")
-        x_rows = [[keep.tile([P, 2, T], F32, name="x_rows_%d_%d" % (z, h)) for h in range(2)] for z in range(PASSES)]
-        tb_rows = [keep.tile([P, 2, V], F32, name="tb_rows_%d" % h) for h in range(2)]
-        xg = [keep.tile([P, PACK, PAD + J], F32, name="xg_%d" % z) for z in range(PASSES)]
+        rw_col = keep.tile([P, 1], F32, name="rw_col")
+        qw_col = keep.tile([P, 1], F32, name="qw_col")
+        identity = keep.tile([P, P], F32, name="identity")
+        x_rows = [
+            [keep.tile([P, hi - lo, T], F32, name="x_rows_%d_%d" % (z, lo)) for lo, hi in X_PIECES[z]]
+            for z in range(PASSES)
+        ]
+        tb_rows = [keep.tile([P, hi - lo, V], F32, name="tb_rows_%d" % lo) for lo, hi in TB_PIECES]
+        xg = [keep.tile([P, PACK, PAD + J], F32, name="xg_%d" % z, tag="xg_%d" % z, align_bytes=64) for z in range(PASSES)]
 
         nc.gpsimd.memset(ws_raw[:].rearrange("p z c -> p (z c)").bitcast(I32), 0)
         nc.gpsimd.memset(wbs_raw[:].bitcast(I32), 0)
+        nc.gpsimd.memset(qw_col[:], 0.0)
+        make_identity(nc, identity[:])
         nc.vector.memset(xg[0][:, :, 0:PAD], 0.0)
         nc.scalar.activation(xg[1][:, :, 0:PAD], xg[0][:, :, 0:PAD], COPY)
 
@@ -61,7 +70,8 @@ def tile_list_steps_abovetable_groupsums_pl_kernel(
         tb_v = tb.rearrange("(p t) c -> p t c", t=PACK)
 
         nc.sync.dma_start(token_list[:], offs)
-        nc.sync.dma_start(w_raw[0][:], w_words[0].rearrange("p c b -> p (c b)").bitcast(I32))
+        nc.sync.dma_start(w_raw[:], w_words.rearrange("z p c b -> p z (c b)").bitcast(I32))
+        nc.sync.dma_start(fk_sb[:], fk.rearrange("(z p t) o -> p z (t o)", z=PASSES, t=PACK))
         for g in range(4):
             nc.sync.dma_start(
                 ws_raw[32 * g : 32 * g + 4, :, :].bitcast(I32),
@@ -69,45 +79,42 @@ def tile_list_steps_abovetable_groupsums_pl_kernel(
             )
         nc.sync.dma_start(x_rows[0][0][:], xf_v[0, :, 0:2, :])
         nc.sync.dma_start(x_rows[0][1][:], xf_v[0, :, 2:4, :])
-        nc.sync.dma_start(x_rows[1][0][:], xf_v[1, :, 0:2, :])
+        nc.sync.dma_start(wb_raw[:].bitcast(I32), wb_words[0].bitcast(I32))
         for g in range(4):
             nc.sync.dma_start(
                 wbs_raw[32 * g : 32 * g + 4, :].bitcast(I32), wb_scales[0, 4 * g : 4 * g + 4, :].bitcast(I32)
             )
-        nc.sync.dma_start(x_rows[1][1][:], xf_v[1, :, 2:4, :])
-        nc.sync.dma_start(w_raw[1][:], w_words[1].rearrange("p c b -> p (c b)").bitcast(I32))
-        nc.sync.dma_start(wb_raw[:].bitcast(I32), wb_words[0].bitcast(I32))
+        nc.sync.dma_start(x_rows[1][0][:], xf_v[1, :, 0:2, :])
         nc.sync.dma_start(entry_list[:], offs2)
-        for h in range(2):
-            nc.sync.dma_start(tb_rows[h][:], tb_v[:, 2 * h : 2 * h + 2, :])
-        nc.gpsimd.dma_start(fk_sb[:], fk.rearrange("(z p t) o -> p z (t o)", z=PASSES, t=PACK))
-        nc.gpsimd.dma_start(rw_sb[:], rw.to_broadcast([P, J]))
-        nc.gpsimd.dma_start(qw_sb[:], qw.to_broadcast([P, Q]))
+        nc.sync.dma_start(x_rows[1][1][:], xf_v[1, :, 2:3, :])
+        nc.sync.dma_start(x_rows[1][2][:], xf_v[1, :, 3:4, :])
+        nc.sync.dma_start(rw_col[:], rw.rearrange("o j -> j o"))
+        nc.sync.dma_start(qw_col[0:Q, :], qw.rearrange("o q -> q o"))
+        for rows_sb, (lo, hi) in zip(tb_rows, TB_PIECES):
+            nc.sync.dma_start(rows_sb[:], tb_v[:, lo:hi, :])
 
-        w_dealt = [keep.tile([P, PACK, P], I32, name="w_dealt_%d" % z, align_bytes=64) for z in range(PASSES)]
         ws_dealt = keep.tile([P, PASSES, PACK, P], U8, name="ws_dealt", align_bytes=64)
-        wb_dealt = keep.tile([P, PACK, P, 2], U8, name="wb_dealt", align_bytes=64)
-        wbs_dealt = keep.tile([P, PACK, P], U8, name="wbs_dealt", align_bytes=64)
+        w_dealt = keep.tile([P, PASSES, PACK, P], I32, name="w_dealt", align_bytes=64)
         nc.vector.tensor_copy(
-            ws_dealt[:].rearrange("p z t m -> p z m t"), ws_raw[:].rearrange("p z (m t) -> p z m t", t=PACK)
+            w_dealt[:].rearrange("p z t (c i) -> p z c t i", i=4),
+            w_raw[:].rearrange("p z (c i t) -> p z c t i", i=4, t=PACK),
+        )
+        nc.vector.tensor_copy(
+            ws_dealt[:], ws_raw[:].rearrange("p z (m t) -> p z t m", t=PACK)
         )
 
         a_bank = psum.tile([P, PACK, J], F32, name="a_bank")
-        steps = [keep.tile([P, PACK, J], F32, name="steps_%d" % z) for z in range(PASSES)]
-        u_bf = [keep.tile([P, J, PACK], BF16, name="u_bf_%d" % z, align_bytes=64) for z in range(PASSES)]
+        steps = [keep.tile([P, PACK, J], F32, name="steps_%d" % z, tag="steps_%d" % z, align_bytes=64) for z in range(PASSES)]
+        u_bf = [keep.tile([P, J, PACK], BF16, name="u_bf_%d" % z, tag="u_bf_%d" % z, align_bytes=64) for z in range(PASSES)]
         u_codes = [keep.tile([P, J], U32, name="u_codes_%d" % z, align_bytes=64) for z in range(PASSES)]
         u_scales = [keep.tile([P, J], U8, name="u_scales_%d" % z, align_bytes=64) for z in range(PASSES)]
 
         def first_stage(z):
-            for h in range(2):
-                for i in range(2):
-                    picked = x_rows[z][h][:, i, :].indirect(token_list[:])
-                    dst = xg[z][:, 2 * h + i, PAD : PAD + J]
-                    if (z, h, i) == (PASSES - 1, 1, 1):
-                        nc.vector.tensor_copy(dst, picked)
-                    else:
-                        nc.scalar.activation(dst, picked, COPY)
-                rows = slice(2 * h, 2 * h + 2)
+            for rows_sb, (lo, hi) in zip(x_rows[z], X_PIECES[z]):
+                for t in range(lo, hi):
+                    picked = rows_sb[:, t - lo, :].indirect(token_list[:])
+                    nc.scalar.activation(xg[z][:, t, PAD : PAD + J], picked, COPY)
+                rows = slice(lo, hi)
                 nc.vector.scalar_tensor_tensor(
                     steps[z][:, rows, :],
                     xg[z][:, rows, PAD - 1 : PAD - 1 + J],
@@ -125,13 +132,10 @@ def tile_list_steps_abovetable_groupsums_pl_kernel(
             nc.vector.quantize_mx(
                 u_codes[z][:].bitcast(E5M2), u_scales[z][:], u_bf[z][:].rearrange("p j t -> p (j t)")
             )
-            nc.vector.tensor_copy(
-                w_dealt[z][:].rearrange("p t m -> p m t"), w_raw[z][:].rearrange("p (m t) -> p m t", t=PACK)
-            )
             for t in range(PACK):
                 nc.tensor.matmul_mx(
                     a_bank[:, t, :],
-                    lhsT=w_dealt[z][:, t, :].bitcast(E5M2),
+                    lhsT=w_dealt[:, z, t, :].bitcast(E5M2),
                     lhsT_scale=ws_dealt[:, z, t, :],
                     rhs=u_codes[z][:].bitcast(E5M2),
                     rhs_scale=u_scales[z][:],
@@ -140,29 +144,31 @@ def tile_list_steps_abovetable_groupsums_pl_kernel(
                 )
 
         first_stage(0)
+        wb_dealt = keep.tile([P, PACK, P, 2], U8, name="wb_dealt", align_bytes=64)
+        wbs_dealt = keep.tile([P, PACK, P], U8, name="wbs_dealt", align_bytes=64)
+        nc.vector.tensor_copy(wbs_dealt[:], wbs_raw[:].rearrange("p (m t) -> p t m", t=PACK))
         nc.vector.tensor_copy(
-            wbs_dealt[:].rearrange("p t m -> p m t"), wbs_raw[:].rearrange("p (m t) -> p m t", t=PACK)
+            wb_dealt[:], wb_raw[:].rearrange("p (m t b) -> p t m b", t=PACK, b=2)
         )
-        slot_weight = keep.tile([P, Q, 2], F32, name="slot_weight")
-        nc.gpsimd.tensor_tensor(
+
+        first_stage(1)
+        spread = psum.tile([P, 2, P], F32, name="spread")
+        qw_sb = keep.tile([P, Q], F32, name="qw_sb")
+        slot_weight = keep.tile([P, Q, 2], F32, name="slot_weight", tag="u_bf_1", align_bytes=64)
+        nc.tensor.transpose(spread[:, 0, :], rw_col[:].to_broadcast([P, P]), identity[:])
+        nc.tensor.transpose(spread[:, 1, :], qw_col[:].to_broadcast([P, P]), identity[:])
+        nc.scalar.copy(qw_sb[:], spread[:, 1, 0:Q])
+        nc.vector.tensor_tensor(
             slot_weight[:],
-            rw_sb[:].rearrange("p (q e) -> p q e", e=2),
+            spread[:, 0, :].rearrange("p (q e) -> p q e", e=2),
             qw_sb[:].unsqueeze(2).to_broadcast([P, Q, 2]),
             ALU.mult,
         )
-        first_stage(1)
-        nc.vector.tensor_copy(
-            wb_dealt[:].rearrange("p t m b -> p m t b"), wb_raw[:].rearrange("p (m t b) -> p m t b", t=PACK, b=2)
-        )
 
         tbg = keep.tile([P, PACK, J], F32, name="tbg")
-        for h in range(2):
-            for i in range(2):
-                picked = tb_rows[h][:, i, :].indirect(entry_list[:])
-                if (h, i) == (1, 1):
-                    nc.vector.tensor_copy(tbg[:, 2 * h + i, :], picked)
-                else:
-                    nc.scalar.activation(tbg[:, 2 * h + i, :], picked, COPY)
+        for rows_sb, (lo, hi) in zip(tb_rows, TB_PIECES):
+            for t in range(lo, hi):
+                nc.scalar.activation(tbg[:, t, :], rows_sb[:, t - lo, :].indirect(entry_list[:]), COPY)
 
         hid_bf = keep.tile([P, J, PACK], BF16, name="hid_bf", align_bytes=64)
         hid_codes = keep.tile([P, J], U32, name="hid_codes", align_bytes=64)
@@ -198,7 +204,9 @@ def tile_list_steps_abovetable_groupsums_pl_kernel(
         even = weighted[:, :, 0, :, :].rearrange("p h q i -> p q h i")
         odd = weighted[:, :, 1, :, :].rearrange("p h q i -> p q h i")
         nc.vector.tensor_tensor(y_bf[:], even, odd, ALU.add)
-        nc.vector.tensor_tensor(y[:].rearrange("p h i q -> p q h i"), even, odd, ALU.add)
+        nc.vector.tensor_tensor(
+            y[:], even.rearrange("p q h i -> p h i q"), odd.rearrange("p q h i -> p h i q"), ALU.add
+        )
         nc.vector.quantize_mx(y_codes[:].bitcast(E4M3), y_scales[:], y_bf[:].rearrange("p q h i -> p (q h i)"))
 
         nc.sync.dma_start(out_0.rearrange("(p t) q -> p (t q)", t=PACK), y[:].rearrange("p h i q -> p (h i q)"))

from contextlib import ExitStack

import concourse.mybir as mybir
from concourse.masks import make_identity

K, T, J, R, V, N, Q = 1024, 512, 128, 512, 512, 512, 64
FLOPS = 2 * K * R * J + 2 * R * N * J

F32 = mybir.dt.float32
BF16 = mybir.dt.bfloat16
I32 = mybir.dt.int32
U32 = mybir.dt.uint32
U16 = mybir.dt.uint16
U8 = mybir.dt.uint8
E5M2 = mybir.dt.float8_e5m2_x4
E4M3 = mybir.dt.float8_e4m3fn_x4
E2M1 = mybir.dt.float4_e2m1fn_x4
ALU = mybir.AluOpType
COPY = mybir.ActivationFunctionType.Copy

P = 128
PACK = 4
PASSES = K // (P * PACK)
PAD = 8
TB_PIECES = ((0, 2), (2, 3), (3, 4))
X_PIECES = (((0, 2), (2, 4)), ((0, 2), (2, 3), (3, 4)))


def walk_planes(ap):
    return ap.rearrange("p t (c i) -> p c t i", i=4)


def walk_words(ap):
    return ap.rearrange("p (c i) t -> p c t i", i=4)


def tile_list_steps_abovetable_groupsums_pl_kernel(
    tc, xf, fk, w_words, w_scales, tb, wb_words, wb_scales, rw, qw, offs, offs2, out_0, out_1, out_2
):
    nc = tc.nc
    with ExitStack() as ctx:
        keep = ctx.enter_context(tc.tile_pool(name="keep", bufs=1))
        psum = ctx.enter_context(tc.psum_pool(name="psum", bufs=1))

        token_list = keep.tile([P, J // 16], U16, name="token_list")
        entry_list = keep.tile([P, J // 16], U16, name="entry_list")
        w_raw = keep.tile([P, PASSES, R], I32, name="w_raw", align_bytes=64)
        ws_raw = keep.tile([P, PASSES, R], U8, name="ws_raw", align_bytes=64)
        wb_raw = keep.tile([P, 2 * N], U8, name="wb_raw", align_bytes=64)
        wbs_raw = keep.tile([P, N], U8, name="wbs_raw", align_bytes=64)
        fk_sb = keep.tile([P, PASSES, PACK], F32, name="fk_sb")
        rw_col = keep.tile([P, 1], F32, name="rw_col")
        qw_col = keep.tile([P, 1], F32, name="qw_col")
        identity = keep.tile([P, P], F32, name="identity")
        x_rows = [
            [keep.tile([P, hi - lo, T], F32, name="x_rows_%d_%d" % (z, lo)) for lo, hi in X_PIECES[z]]
            for z in range(PASSES)
        ]
        tb_rows = [keep.tile([P, hi - lo, V], F32, name="tb_rows_%d" % lo) for lo, hi in TB_PIECES]
        xg = [keep.tile([P, PACK, PAD + J], F32, name="xg_%d" % z, tag="xg_%d" % z, align_bytes=64) for z in range(PASSES)]

        nc.gpsimd.memset(ws_raw[:].rearrange("p z c -> p (z c)").bitcast(I32), 0)
        nc.gpsimd.memset(wbs_raw[:].bitcast(I32), 0)
        nc.gpsimd.memset(qw_col[:], 0.0)
        make_identity(nc, identity[:])
        nc.vector.memset(xg[0][:, :, 0:PAD], 0.0)
        nc.scalar.activation(xg[1][:, :, 0:PAD], xg[0][:, :, 0:PAD], COPY)

        xf_v = xf.rearrange("(z p t) c -> z p t c", z=PASSES, t=PACK)
        tb_v = tb.rearrange("(p t) c -> p t c", t=PACK)

        nc.sync.dma_start(token_list[:], offs)
        nc.sync.dma_start(w_raw[:], w_words.rearrange("z p c b -> p z (c b)").bitcast(I32))
        nc.sync.dma_start(fk_sb[:], fk.rearrange("(z p t) o -> p z (t o)", z=PASSES, t=PACK))
        for g in range(4):
            nc.sync.dma_start(
                ws_raw[32 * g : 32 * g + 4, :, :].bitcast(I32),
                w_scales[:, 4 * g : 4 * g + 4, :].rearrange("z r c -> r z c").bitcast(I32),
            )
        nc.sync.dma_start(x_rows[0][0][:], xf_v[0, :, 0:2, :])
        nc.sync.dma_start(x_rows[0][1][:], xf_v[0, :, 2:4, :])
        nc.sync.dma_start(wb_raw[:].bitcast(I32), wb_words[0].bitcast(I32))
        for g in range(4):
            nc.sync.dma_start(
                wbs_raw[32 * g : 32 * g + 4, :].bitcast(I32), wb_scales[0, 4 * g : 4 * g + 4, :].bitcast(I32)
            )
        nc.sync.dma_start(x_rows[1][0][:], xf_v[1, :, 0:2, :])
        nc.sync.dma_start(entry_list[:], offs2)
        nc.sync.dma_start(x_rows[1][1][:], xf_v[1, :, 2:3, :])
        nc.sync.dma_start(x_rows[1][2][:], xf_v[1, :, 3:4, :])
        nc.sync.dma_start(rw_col[:], rw.rearrange("o j -> j o"))
        nc.sync.dma_start(qw_col[0:Q, :], qw.rearrange("o q -> q o"))
        for rows_sb, (lo, hi) in zip(tb_rows, TB_PIECES):
            nc.sync.dma_start(rows_sb[:], tb_v[:, lo:hi, :])

        ws_dealt = keep.tile([P, PASSES, PACK, P], U8, name="ws_dealt", align_bytes=64)
        w_dealt = keep.tile([P, PASSES, PACK, P], I32, name="w_dealt", align_bytes=64)
        nc.vector.tensor_copy(
            w_dealt[:].rearrange("p z t (c i) -> p z c t i", i=4),
            w_raw[:].rearrange("p z (c i t) -> p z c t i", i=4, t=PACK),
        )
        nc.vector.tensor_copy(
            ws_dealt[:], ws_raw[:].rearrange("p z (m t) -> p z t m", t=PACK)
        )

        a_bank = psum.tile([P, PACK, J], F32, name="a_bank")
        steps = [keep.tile([P, PACK, J], F32, name="steps_%d" % z, tag="steps_%d" % z, align_bytes=64) for z in range(PASSES)]
        u_bf = [keep.tile([P, J, PACK], BF16, name="u_bf_%d" % z, tag="u_bf_%d" % z, align_bytes=64) for z in range(PASSES)]
        u_codes = [keep.tile([P, J], U32, name="u_codes_%d" % z, align_bytes=64) for z in range(PASSES)]
        u_scales = [keep.tile([P, J], U8, name="u_scales_%d" % z, align_bytes=64) for z in range(PASSES)]

        def first_stage(z):
            for rows_sb, (lo, hi) in zip(x_rows[z], X_PIECES[z]):
                for t in range(lo, hi):
                    picked = rows_sb[:, t - lo, :].indirect(token_list[:])
                    nc.scalar.activation(xg[z][:, t, PAD : PAD + J], picked, COPY)
                rows = slice(lo, hi)
                nc.vector.scalar_tensor_tensor(
                    steps[z][:, rows, :],
                    xg[z][:, rows, PAD - 1 : PAD - 1 + J],
                    -0.6,
                    xg[z][:, rows, PAD : PAD + J],
                    ALU.mult,
                    ALU.add,
                )
            nc.vector.tensor_tensor(
                walk_words(u_bf[z][:]),
                walk_planes(steps[z][:]),
                fk_sb[:, z, :].unsqueeze(1).unsqueeze(3).to_broadcast([P, J // 4, PACK, 4]),
                ALU.mult,
            )
            nc.vector.quantize_mx(
                u_codes[z][:].bitcast(E5M2), u_scales[z][:], u_bf[z][:].rearrange("p j t -> p (j t)")
            )
            for t in range(PACK):
                nc.tensor.matmul_mx(
                    a_bank[:, t, :],
                    lhsT=w_dealt[:, z, t, :].bitcast(E5M2),
                    lhsT_scale=ws_dealt[:, z, t, :],
                    rhs=u_codes[z][:].bitcast(E5M2),
                    rhs_scale=u_scales[z][:],
                    start=(z == 0 and t == 0),
                    stop=(z == PASSES - 1 and t == PACK - 1),
                )

        first_stage(0)
        wb_dealt = keep.tile([P, PACK, P, 2], U8, name="wb_dealt", align_bytes=64)
        wbs_dealt = keep.tile([P, PACK, P], U8, name="wbs_dealt", align_bytes=64)
        nc.vector.tensor_copy(wbs_dealt[:], wbs_raw[:].rearrange("p (m t) -> p t m", t=PACK))
        nc.vector.tensor_copy(
            wb_dealt[:], wb_raw[:].rearrange("p (m t b) -> p t m b", t=PACK, b=2)
        )

        first_stage(1)
        spread = psum.tile([P, 2, P], F32, name="spread")
        qw_sb = keep.tile([P, Q], F32, name="qw_sb")
        slot_weight = keep.tile([P, Q, 2], F32, name="slot_weight", tag="u_bf_1", align_bytes=64)
        nc.tensor.transpose(spread[:, 0, :], rw_col[:].to_broadcast([P, P]), identity[:])
        nc.tensor.transpose(spread[:, 1, :], qw_col[:].to_broadcast([P, P]), identity[:])
        nc.scalar.copy(qw_sb[:], spread[:, 1, 0:Q])
        nc.vector.tensor_tensor(
            slot_weight[:],
            spread[:, 0, :].rearrange("p (q e) -> p q e", e=2),
            qw_sb[:].unsqueeze(2).to_broadcast([P, Q, 2]),
            ALU.mult,
        )

        tbg = keep.tile([P, PACK, J], F32, name="tbg")
        for rows_sb, (lo, hi) in zip(tb_rows, TB_PIECES):
            for t in range(lo, hi):
                nc.scalar.activation(tbg[:, t, :], rows_sb[:, t - lo, :].indirect(entry_list[:]), COPY)

        hid_bf = keep.tile([P, J, PACK], BF16, name="hid_bf", align_bytes=64)
        hid_codes = keep.tile([P, J], U32, name="hid_codes", align_bytes=64)
        hid_scales = keep.tile([P, J], U8, name="hid_scales", align_bytes=64)
        nc.vector.tensor_tensor(walk_words(hid_bf[:]), walk_planes(a_bank[:]), walk_planes(tbg[:]), ALU.max)
        nc.vector.quantize_mx(hid_codes[:].bitcast(E5M2), hid_scales[:], hid_bf[:].rearrange("p j t -> p (j t)"))

        weighted = keep.tile([P, 2, 2, Q, 2], F32, name="weighted")
        for h in range(2):
            p_bank = psum.tile([P, 2, J], F32, name="p_bank_%d" % h)
            for i in range(2):
                t = 2 * h + i
                nc.tensor.matmul_mx(
                    p_bank[:, i, :],
                    lhsT=wb_dealt[:, t, :, :].rearrange("p m b -> p (m b)").bitcast(E2M1),
                    lhsT_scale=wbs_dealt[:, t, :],
                    rhs=hid_codes[:].bitcast(E5M2),
                    rhs_scale=hid_scales[:],
                    start=True,
                    stop=True,
                )
            nc.vector.tensor_tensor(
                weighted[:, h, :, :, :],
                p_bank[:].rearrange("p i (q e) -> p e q i", e=2),
                slot_weight[:].rearrange("p q e -> p e q").unsqueeze(3).to_broadcast([P, 2, Q, 2]),
                ALU.mult,
            )

        y_bf = keep.tile([P, Q, 2, 2], BF16, name="y_bf", align_bytes=64)
        y = keep.tile([P, 2, 2, Q], F32, name="y")
        y_codes = keep.tile([P, Q], U32, name="y_codes", align_bytes=64)
        y_scales = keep.tile([P, Q], U8, name="y_scales", align_bytes=64)
        even = weighted[:, :, 0, :, :].rearrange("p h q i -> p q h i")
        odd = weighted[:, :, 1, :, :].rearrange("p h q i -> p q h i")
        nc.vector.tensor_tensor(y_bf[:], even, odd, ALU.add)
        nc.vector.tensor_tensor(
            y[:], even.rearrange("p q h i -> p h i q"), odd.rearrange("p q h i -> p h i q"), ALU.add
        )
        nc.vector.quantize_mx(y_codes[:].bitcast(E4M3), y_scales[:], y_bf[:].rearrange("p q h i -> p (q h i)"))

        nc.sync.dma_start(out_0.rearrange("(p t) q -> p (t q)", t=PACK), y[:].rearrange("p h i q -> p (h i q)"))
        nc.scalar.dma_start(out_1[0].rearrange("p c b -> p (c b)").bitcast(I32), y_codes[:].bitcast(I32))
        for g in range(4):
            queue = nc.sync if g % 2 == 0 else nc.scalar
            queue.dma_start(
                out_2[0, 4 * g : 4 * g + 4, :].bitcast(I32), y_scales[32 * g : 32 * g + 4, :].bitcast(I32)
            )
